import numpy as np
import ml_dtypes


def mxq(x, axis, fmt="e4m3"):
    dtype, down = {"e4m3": (ml_dtypes.float8_e4m3fn, 7), "e5m2": (ml_dtypes.float8_e5m2, 14)}[fmt]
    v = np.moveaxis(np.asarray(x, np.float32).astype(ml_dtypes.bfloat16).astype(np.float64), axis, -1)
    blocks = v.reshape(v.shape[:-1] + (-1, 32))
    amax = np.abs(blocks).max(-1, keepdims=True)
    byte = np.maximum(np.where(amax > 0, np.frexp(amax)[1] - 1 + 127, 0) - down, 1)
    scale = np.exp2(byte - 127.0)
    codes = (blocks / scale).astype(np.float32).astype(dtype).astype(np.float64)
    return np.moveaxis((codes * scale).reshape(v.shape), -1, axis)


WIDE = False


def mx_kscale(k):
    if not WIDE:
        return np.ones(k)
    levels = np.array([30, -30])
    if k % 512:
        return np.exp2(np.random.permutation(np.resize(levels, k // 32))).repeat(32)
    a = np.empty((k // 512, 16))
    for p in range(k // 512):
        a[p, :8] = np.random.permutation(np.resize(levels, 8))
        for g in range(8):
            far = levels[np.abs(levels - a[p, g]) >= 10]
            a[p, g + 8] = far[np.random.randint(len(far))]
    return np.exp2(a.ravel()).repeat(32)


BF16 = ml_dtypes.bfloat16


def bf(x):
    return np.asarray(x, np.float32).astype(BF16)


def f64(x):
    return np.asarray(x).astype(np.float64)


M, N, KS, KT = 2048, 1536, 1024, 512

TAIL = 0.7


def setup_inputs():
    s = np.concatenate([mx_kscale(KS), mx_kscale(KT)])
    phi = 0.25 * np.random.standard_normal((M, N))
    phi[:, KS:] *= np.exp(TAIL * np.random.standard_normal((M, KT)) - TAIL ** 2)
    p = 2.0 * np.random.standard_normal((N, N)) / np.sqrt(N)
    return {"phi": bf(phi * s),
            "p": bf(p / s[:, None] / s),
            "w": bf(0.5 + np.random.random_sample(M))}


def reference(phi, p, w):
    phi, p, w = f64(phi), f64(p), f64(w)
    x = ((mxq(phi[:, :KS], 1, "e4m3") @ mxq(p[:KS], 0, "e4m3"))
         + (mxq(phi[:, KS:], 1, "e5m2") @ mxq(p[KS:], 0, "e4m3")))
    return w * np.sum(x * phi, axis=1)

@@ -1,0 +1,286 @@
+from contextlib import ExitStack
+
+import concourse.mybir as mybir
+from concourse.masks import make_identity
+
+F32 = mybir.dt.float32
+BF16 = mybir.dt.bfloat16
+U32 = mybir.dt.uint32
+U8 = mybir.dt.uint8
+E4M3 = mybir.dt.float8_e4m3fn_x4
+E5M2 = mybir.dt.float8_e5m2_x4
+ALU = mybir.AluOpType
+
+M, N = 2048, 1536
+FLOPS = 2 * M * N * N
+P = 128
+TILES = M // P
+K_PASS = 512
+PASSES = N // K_PASS
+COLS = 512
+BLOCKS = N // COLS
+HEAD = 4
+V_COLS = (320, 192, 0)
+
+
+def tile_transition_density_grid_s2_kernel(tc, phi, p, w, out):
+    nc = tc.nc
+    phi_rows = phi.rearrange("(p t) n -> p t n", t=TILES)
+    p_rows = p.rearrange("(g p j) n -> g p j n", p=P, j=4)
+
+    with ExitStack() as ctx:
+        keep = ctx.enter_context(tc.tile_pool(name="keep", bufs=1))
+        stage = ctx.enter_context(tc.tile_pool(name="stage", bufs=3))
+        junk = ctx.enter_context(tc.tile_pool(name="junk", bufs=3))
+        turns = ctx.enter_context(tc.psum_pool(name="turns", bufs=3))
+        sums = ctx.enter_context(tc.psum_pool(name="sums", bufs=5))
+        ctx.enter_context(tc.manual_schedule())
+
+        warm = keep.tile([P, 2], F32, name="warm")
+        nc.vector.memset(warm[:], 0.0)
+        nc.scalar.copy(out=warm[:, 1:2], in_=warm[:, 0:1])
+        ident = keep.tile([P, P], F32, name="ident", align_bytes=64)
+        make_identity(nc, ident[:])
+
+        head_phi = [keep.tile([P, HEAD, K_PASS], BF16, name="head_phi%d" % g, align_bytes=64) for g in range(PASSES)]
+        p_raw = {}
+        for b in range(BLOCKS):
+            for g in range(PASSES):
+                p_raw[g, b] = keep.tile([P, 4, COLS], BF16, name="p_raw_%d_%d" % (g, b), align_bytes=64)
+        pair_phi = {}
+        for k in range(2, TILES // 2):
+            pair_phi[k] = keep.tile([P, 2, N], BF16, name="pair_phi%d" % k, align_bytes=64)
+        def load_head(g):
+            cols = slice(g * K_PASS, (g + 1) * K_PASS)
+            for t in range(0, HEAD, 2):
+                nc.sync.dma_start(out=head_phi[g][:, t : t + 2, :], in_=phi_rows[:, t : t + 2, cols])
+
+        def load_pair(k):
+            nc.sync.dma_start(out=pair_phi[k][:], in_=phi_rows[:, 2 * k : 2 * k + 2, :])
+
+        def load_p(g, b):
+            nc.sync.dma_start(out=p_raw[g, b][:], in_=p_rows[g, :, :, b * COLS : (b + 1) * COLS])
+
+        w_sb = keep.tile([P, TILES], BF16, name="w_sb")
+        for g in range(PASSES):
+            load_head(g)
+            load_p(g, 0)
+        load_pair(2)
+        nc.sync.dma_start(out=w_sb[:], in_=w.rearrange("(p t) -> p t", t=TILES))
+        load_pair(3)
+        load_pair(4)
+        load_p(0, 1)
+        load_pair(5)
+        load_p(1, 1)
+        load_p(2, 1)
+        for g in range(PASSES):
+            load_p(g, 2)
+        load_pair(6)
+        load_pair(7)
+
+        def phi_part(t, g):
+            if t < HEAD:
+                return head_phi[g][:, t, :]
+            return pair_phi[t // 2][:, t % 2, g * K_PASS : (g + 1) * K_PASS]
+
+        p_codes = {}
+        p_scales = {}
+        p_grouped = {}
+
+        def p_source(g, b, c0, c1):
+            return p_raw[g, b][:, :, c0:c1]
+
+        def p_interleave(engine, g, b, c0, c1):
+            if (g, b) not in p_grouped:
+                p_grouped[g, b] = stage.tile([P, 4 * COLS], BF16, name="p_grouped", align_bytes=64)
+            dst = p_grouped[g, b][:, 4 * c0 : 4 * c1].rearrange("p (c i t) -> p c t i", i=4, t=4)
+            src = p_source(g, b, c0, c1).rearrange("p t (c i) -> p c t i", i=4)
+            if engine == "v":
+                nc.vector.tensor_copy(out=dst, in_=src)
+            else:
+                nc.scalar.copy(out=dst, in_=src)
+
+        def p_quantize(g, b):
+            codes = keep.tile([P, COLS], U32, name="p_codes_%d_%d" % (g, b), align_bytes=64)
+            scales = keep.tile([P, COLS], U8, name="p_scales_%d_%d" % (g, b), align_bytes=64)
+            nc.vector.quantize_mx(out=codes[:].bitcast(E4M3), scales=scales[:], in_=p_grouped[g, b][:])
+            p_codes[g, b] = codes
+            p_scales[g, b] = scales
+
+        phi_codes = {}
+        phi_scales = {}
+
+        split = {}
+
+        def split_words(k, i):
+            if k not in split:
+                split[k] = stage.tile([P, 2, PASSES, 2, P], F32, name="split", align_bytes=64)
+            nc.scalar.copy(
+                out=split[k][:, i, :, :, :],
+                in_=pair_phi[k][:, i, :].bitcast(F32).rearrange("p (g m u) -> p g u m", g=PASSES, u=2),
+            )
+
+        def turn(tiles, g):
+            bank = turns.tile([P, 2, 2, P], F32, name="bank")
+            for i in range(2):
+                if tiles[i] // 2 in split:
+                    halves = [split[tiles[i] // 2][:, i, g, u, :] for u in range(2)]
+                else:
+                    words = phi_part(tiles[i], g).bitcast(F32)
+                    halves = [words[:, u : K_PASS // 2 : 2] for u in range(2)]
+                for u in range(2):
+                    nc.tensor.transpose(bank[:, i, u, :], halves[u], ident[:])
+            return bank
+
+        def empty(bank, dst):
+            nc.scalar.copy(
+                out=dst.bitcast(F32).rearrange("p (i r u) -> p i r u", i=2, u=2),
+                in_=bank[:].rearrange("p i u r -> p i r u"),
+            )
+
+        def quantize_phi(src, n_tiles, fmt, label):
+            codes = keep.tile([P, n_tiles * P], U32, name="phi_codes_" + label, align_bytes=64)
+            scales = keep.tile([P, n_tiles * P], U8, name="phi_scales_" + label, align_bytes=64)
+            nc.vector.quantize_mx(out=codes[:].bitcast(fmt), scales=scales[:], in_=src)
+            return codes, scales
+
+        accs = {}
+
+        def mult(t, b, passes=(0, 1, 2)):
+            if 0 in passes:
+                accs[t, b] = sums.tile([P, COLS], F32, name="acc")
+            for g in passes:
+                codes, scales, col, fmt = phi_codes[t, g]
+                nc.tensor.matmul_mx(
+                    out=accs[t, b][:],
+                    lhsT=codes[:, col : col + P].bitcast(fmt),
+                    lhsT_scale=scales[:, col : col + P],
+                    rhs=p_codes[g, b][:].bitcast(E4M3),
+                    rhs_scale=p_scales[g, b][:],
+                    start=(g == 0),
+                    stop=(g == PASSES - 1),
+                )
+
+        parts = keep.tile([P, TILES, BLOCKS], F32, name="parts")
+
+        def dot(t, b):
+            product = junk.tile([P, COLS], F32, name="product")
+            nc.vector.scalar_tensor_tensor(
+                out=product[:],
+                in0=accs[t, b][:],
+                scalar=w_sb[:, t : t + 1],
+                in1=phi_part(t, b),
+                op0=ALU.mult,
+                op1=ALU.mult,
+                accum_out=parts[:, t, b : b + 1],
+            )
+
+        pair_grouped = {}
+
+        def pair_turn(k):
+            pair_grouped[k] = stage.tile([P, 3 * 2 * P * 4], BF16, name="pair_grouped", align_bytes=64)
+            for g in range(PASSES):
+                bank = turn((2 * k, 2 * k + 1), g)
+                empty(bank, pair_grouped[k][:, 1024 * g : 1024 * (g + 1)])
+
+        def pair_quantize(k, which):
+            if which == 0:
+                codes, scales = quantize_phi(pair_grouped[k][:, 0:2048], 4, E4M3, "a%d" % k)
+                for i in range(2):
+                    for g in range(2):
+                        phi_codes[2 * k + i, g] = (codes, scales, (2 * g + i) * P, E4M3)
+            else:
+                codes, scales = quantize_phi(pair_grouped[k][:, 2048:3072], 2, E5M2, "b%d" % k)
+                for i in range(2):
+                    phi_codes[2 * k + i, 2] = (codes, scales, i * P, E5M2)
+
+        def head_turn(g):
+            grouped = stage.tile([P, HEAD * P * 4], BF16, name="head_grouped", align_bytes=64)
+            for h in range(2):
+                bank = turn((2 * h, 2 * h + 1), g)
+                empty(bank, grouped[:, 1024 * h : 1024 * (h + 1)])
+            return grouped
+
+        def head_quantize(grouped, g):
+            fmt = E4M3 if g < 2 else E5M2
+            codes, scales = quantize_phi(grouped[:], HEAD, fmt, "h%d" % g)
+            for t in range(HEAD):
+                phi_codes[t, g] = (codes, scales, t * P, fmt)
+
+        def p_head(g):
+            p_interleave("v", g, 0, 0, V_COLS[0])
+            p_interleave("s", g, 0, V_COLS[0], COLS)
+
+        g0 = head_turn(0)
+        p_head(0)
+        head_quantize(g0, 0)
+        p_quantize(0, 0)
+        g1 = head_turn(1)
+        p_head(1)
+        head_quantize(g1, 1)
+        p_quantize(1, 0)
+        for t in range(HEAD):
+            mult(t, 0, (0,))
+        g2 = head_turn(2)
+        p_head(2)
+        head_quantize(g2, 2)
+        p_quantize(2, 0)
+        for t in range(HEAD):
+            mult(t, 0, (1,))
+        pair_turn(2)
+        pair_quantize(2, 0)
+        pair_quantize(2, 1)
+        for t in range(HEAD):
+            mult(t, 0, (2,))
+            dot(t, 0)
+        pair_turn(3)
+        pair_quantize(3, 0)
+        pair_quantize(3, 1)
+
+        def p_copies(g, b):
+            c0 = V_COLS[b]
+            cut = c0 + (COLS - c0) // 2
+            calls = [
+                lambda: p_interleave("s", g, b, c0, cut),
+                lambda: p_interleave("s", g, b, cut, COLS),
+            ]
+            if c0:
+                calls.append(lambda: p_interleave("v", g, b, 0, c0))
+            return calls
+
+        def p_codes_of(g, b):
+            return [lambda: p_quantize(g, b)]
+
+        def split_chores(k):
+            return [lambda: split_words(k, 0), lambda: split_words(k, 1)]
+
+        def rounds(k, groups, chores):
+            if k is not None:
+                pair_turn(k)
+            marks = [(n + 1) * len(chores) // len(groups) for n in range(len(groups))]
+            done = 0
+            for n in range(len(groups)):
+                mult(groups[n][0], groups[n][1])
+                for call in chores[done : marks[n]]:
+                    call()
+                done = marks[n]
+                dot(groups[n][0], groups[n][1])
+                if k is not None and n < 2:
+                    pair_quantize(k, n)
+
+        def grid(tiles, b):
+            return [(t, b) for t in tiles]
+
+        rounds(4, grid((4, 5), 0), p_copies(0, 1))
+        rounds(5, grid((6, 7), 0), p_codes_of(0, 1) + p_copies(1, 1))
+        rounds(None, grid((8, 9), 0), p_codes_of(1, 1) + p_copies(2, 1))
+        rounds(None, grid((10, 11), 0), p_codes_of(2, 1) + split_chores(6))
+        rounds(None, grid(range(0, 4), 1), p_copies(0, 2))
+        rounds(6, grid(range(4, 8), 1), p_codes_of(0, 2) + split_chores(7) + p_copies(1, 2))
+        rounds(7, grid((12, 13), 0) + grid((8, 9), 1), p_codes_of(1, 2) + p_copies(2, 2))
+        rounds(None, grid((14, 15), 0) + grid(range(10, 16), 1), p_codes_of(2, 2))
+        rounds(None, grid(range(TILES), 2), [])
+
+        rho = keep.tile([P, TILES], F32, name="rho")
+        nc.vector.tensor_reduce(out=rho[:], in_=parts[:], op=ALU.add, axis=mybir.AxisListType.X)
+        nc.sync.dma_start(out=out.rearrange("(p t) -> p t", t=TILES), in_=rho[:])

@@ -20,7 +20,7 @@ PASSES = N // K_PASS
 COLS = 512
 BLOCKS = N // COLS
 HEAD = 4
-V_COLS = (320, 192, 0)
+V_COLS = (320, 0, 0)
 
 
 def tile_transition_density_grid_s2_kernel(tc, phi, p, w, out):
@@ -146,6 +146,14 @@ def tile_transition_density_grid_s2_kernel(tc, phi, p, w, out):
 
         accs = {}
 
+        zeros = keep.tile([P, COLS], BF16, name="zeros", align_bytes=64)
+        nc.vector.memset(zeros[:], 0.0)
+
+        def keep_clock(n):
+            acc = sums.tile([P, COLS], F32, name="acc")
+            for i in range(n):
+                nc.tensor.matmul(acc[:], lhsT=zeros[:, 0:P], rhs=zeros[:], start=True, stop=True)
+
         def mult(t, b, passes=(0, 1, 2)):
             if 0 in passes:
                 accs[t, b] = sums.tile([P, COLS], F32, name="acc")
@@ -198,6 +206,8 @@ def tile_transition_density_grid_s2_kernel(tc, phi, p, w, out):
             grouped = stage.tile([P, HEAD * P * 4], BF16, name="head_grouped", align_bytes=64)
             for h in range(2):
                 bank = turn((2 * h, 2 * h + 1), g)
+                if g == 1:
+                    keep_clock(1)
                 empty(bank, grouped[:, 1024 * h : 1024 * (h + 1)])
             return grouped
 
@@ -211,7 +221,9 @@ def tile_transition_density_grid_s2_kernel(tc, phi, p, w, out):
             p_interleave("v", g, 0, 0, V_COLS[0])
             p_interleave("s", g, 0, V_COLS[0], COLS)
 
+        keep_clock(6)
         g0 = head_turn(0)
+        keep_clock(3)
         p_head(0)
         head_quantize(g0, 0)
         p_quantize(0, 0)
@@ -268,18 +280,28 @@ def tile_transition_density_grid_s2_kernel(tc, phi, p, w, out):
                 if k is not None and n < 2:
                     pair_quantize(k, n)
 
+        def by_pass(tiles, b, chores):
+            for g in range(PASSES):
+                for t in tiles:
+                    mult(t, b, (g,))
+                    if g == PASSES - 1:
+                        dot(t, b)
+                for call in chores[g]:
+                    call()
+
         def grid(tiles, b):
             return [(t, b) for t in tiles]
 
         rounds(4, grid((4, 5), 0), p_copies(0, 1))
         rounds(5, grid((6, 7), 0), p_codes_of(0, 1) + p_copies(1, 1))
         rounds(None, grid((8, 9), 0), p_codes_of(1, 1) + p_copies(2, 1))
-        rounds(None, grid((10, 11), 0), p_codes_of(2, 1) + split_chores(6))
-        rounds(None, grid(range(0, 4), 1), p_copies(0, 2))
+        rounds(None, grid((10, 11), 0), split_chores(6))
+        by_pass(range(0, 4), 1, (p_codes_of(2, 1), [], p_copies(0, 2)))
         rounds(6, grid(range(4, 8), 1), p_codes_of(0, 2) + split_chores(7) + p_copies(1, 2))
         rounds(7, grid((12, 13), 0) + grid((8, 9), 1), p_codes_of(1, 2) + p_copies(2, 2))
         rounds(None, grid((14, 15), 0) + grid(range(10, 16), 1), p_codes_of(2, 2))
-        rounds(None, grid(range(TILES), 2), [])
+        by_pass(range(0, 4), 2, ([], [], []))
+        rounds(None, grid(range(4, TILES), 2), [])
 
         rho = keep.tile([P, TILES], F32, name="rho")
         nc.vector.tensor_reduce(out=rho[:], in_=parts[:], op=ALU.add, axis=mybir.AxisListType.X)

@@ -295,13 +295,15 @@ def tile_transition_density_grid_s2_kernel(tc, phi, p, w, out):
         rounds(4, grid((4, 5), 0), p_copies(0, 1))
         rounds(5, grid((6, 7), 0), p_codes_of(0, 1) + p_copies(1, 1))
         rounds(None, grid((8, 9), 0), p_codes_of(1, 1) + p_copies(2, 1))
-        rounds(None, grid((10, 11), 0), split_chores(6))
+        rounds(None, grid((10, 11), 0), [])
         by_pass(range(0, 4), 1, (p_codes_of(2, 1), [], p_copies(0, 2)))
-        rounds(6, grid(range(4, 8), 1), p_codes_of(0, 2) + split_chores(7) + p_copies(1, 2))
-        rounds(7, grid((12, 13), 0) + grid((8, 9), 1), p_codes_of(1, 2) + p_copies(2, 2))
-        rounds(None, grid((14, 15), 0) + grid(range(10, 16), 1), p_codes_of(2, 2))
-        by_pass(range(0, 4), 2, ([], [], []))
-        rounds(None, grid(range(4, TILES), 2), [])
+        rounds(None, grid(range(4, 8), 1), p_copies(1, 2) + p_codes_of(0, 2))
+        rounds(None, grid(range(8, 12), 1), p_codes_of(1, 2) + p_copies(2, 2) + split_chores(6))
+        by_pass(range(0, 4), 2, (p_codes_of(2, 2), [], split_chores(7)))
+        rounds(6, grid(range(4, 8), 2), [])
+        rounds(7, grid(range(8, 12), 2), [])
+        for t in range(12, TILES):
+            rounds(None, [(t, b) for b in range(BLOCKS)], [])
 
         rho = keep.tile([P, TILES], F32, name="rho")
         nc.vector.tensor_reduce(out=rho[:], in_=parts[:], op=ALU.add, axis=mybir.AxisListType.X)

@@ -39,17 +39,17 @@ def tile_transition_density_grid_s2_kernel(tc, phi, p, w, out):
         warm = keep.tile([P, 2], F32, name="warm")
         nc.vector.memset(warm[:], 0.0)
         nc.scalar.copy(out=warm[:, 1:2], in_=warm[:, 0:1])
-        ident = keep.tile([P, P], F32, name="ident", align_bytes=64)
+        ident = keep.tile([P, P], F32, name="ident", align_bytes=256)
         make_identity(nc, ident[:])
 
-        head_phi = [keep.tile([P, HEAD, K_PASS], BF16, name="head_phi%d" % g, align_bytes=64) for g in range(PASSES)]
+        head_phi = [keep.tile([P, HEAD, K_PASS], BF16, name="head_phi%d" % g, align_bytes=256) for g in range(PASSES)]
         p_raw = {}
         for b in range(BLOCKS):
             for g in range(PASSES):
-                p_raw[g, b] = keep.tile([P, 4, COLS], BF16, name="p_raw_%d_%d" % (g, b), align_bytes=64)
+                p_raw[g, b] = keep.tile([P, 4, COLS], BF16, name="p_raw_%d_%d" % (g, b), align_bytes=256)
         pair_phi = {}
         for k in range(2, TILES // 2):
-            pair_phi[k] = keep.tile([P, 2, N], BF16, name="pair_phi%d" % k, align_bytes=64)
+            pair_phi[k] = keep.tile([P, 2, N], BF16, name="pair_phi%d" % k, align_bytes=256)
         def load_head(g):
             cols = slice(g * K_PASS, (g + 1) * K_PASS)
             for t in range(0, HEAD, 2):
@@ -92,7 +92,7 @@ def tile_transition_density_grid_s2_kernel(tc, phi, p, w, out):
 
         def p_interleave(engine, g, b, c0, c1):
             if (g, b) not in p_grouped:
-                p_grouped[g, b] = stage.tile([P, 4 * COLS], BF16, name="p_grouped", align_bytes=64)
+                p_grouped[g, b] = stage.tile([P, 4 * COLS], BF16, name="p_grouped", align_bytes=256)
             dst = p_grouped[g, b][:, 4 * c0 : 4 * c1].rearrange("p (c i t) -> p c t i", i=4, t=4)
             src = p_source(g, b, c0, c1).rearrange("p t (c i) -> p c t i", i=4)
             if engine == "v":
@@ -101,8 +101,8 @@ def tile_transition_density_grid_s2_kernel(tc, phi, p, w, out):
                 nc.scalar.copy(out=dst, in_=src)
 
         def p_quantize(g, b):
-            codes = keep.tile([P, COLS], U32, name="p_codes_%d_%d" % (g, b), align_bytes=64)
-            scales = keep.tile([P, COLS], U8, name="p_scales_%d_%d" % (g, b), align_bytes=64)
+            codes = keep.tile([P, COLS], U32, name="p_codes_%d_%d" % (g, b), align_bytes=256)
+            scales = keep.tile([P, COLS], U8, name="p_scales_%d_%d" % (g, b), align_bytes=256)
             nc.vector.quantize_mx(out=codes[:].bitcast(E4M3), scales=scales[:], in_=p_grouped[g, b][:])
             p_codes[g, b] = codes
             p_scales[g, b] = scales
@@ -114,7 +114,7 @@ def tile_transition_density_grid_s2_kernel(tc, phi, p, w, out):
 
         def split_words(k, i):
             if k not in split:
-                split[k] = stage.tile([P, 2, PASSES, 2, P], F32, name="split", align_bytes=64)
+                split[k] = stage.tile([P, 2, PASSES, 2, P], F32, name="split", align_bytes=256)
             nc.scalar.copy(
                 out=split[k][:, i, :, :, :],
                 in_=pair_phi[k][:, i, :].bitcast(F32).rearrange("p (g m u) -> p g u m", g=PASSES, u=2),
@@ -139,14 +139,14 @@ def tile_transition_density_grid_s2_kernel(tc, phi, p, w, out):
             )
 
         def quantize_phi(src, n_tiles, fmt, label):
-            codes = keep.tile([P, n_tiles * P], U32, name="phi_codes_" + label, align_bytes=64)
-            scales = keep.tile([P, n_tiles * P], U8, name="phi_scales_" + label, align_bytes=64)
+            codes = keep.tile([P, n_tiles * P], U32, name="phi_codes_" + label, align_bytes=256)
+            scales = keep.tile([P, n_tiles * P], U8, name="phi_scales_" + label, align_bytes=256)
             nc.vector.quantize_mx(out=codes[:].bitcast(fmt), scales=scales[:], in_=src)
             return codes, scales
 
         accs = {}
 
-        zeros = keep.tile([P, COLS], BF16, name="zeros", align_bytes=64)
+        zeros = keep.tile([P, COLS], BF16, name="zeros", align_bytes=256)
         nc.vector.memset(zeros[:], 0.0)
 
         def keep_clock(n):
@@ -176,7 +176,7 @@ def tile_transition_density_grid_s2_kernel(tc, phi, p, w, out):
             nc.vector.scalar_tensor_tensor(
                 out=product[:],
                 in0=accs[t, b][:],
-                scalar=w_sb[:, t : t + 1],
+                scalar=w_sb[:, t : t + 1] if t == TILES - 1 else 1.0,
                 in1=phi_part(t, b),
                 op0=ALU.mult,
                 op1=ALU.mult,
@@ -186,7 +186,7 @@ def tile_transition_density_grid_s2_kernel(tc, phi, p, w, out):
         pair_grouped = {}
 
         def pair_turn(k):
-            pair_grouped[k] = stage.tile([P, 3 * 2 * P * 4], BF16, name="pair_grouped", align_bytes=64)
+            pair_grouped[k] = stage.tile([P, 3 * 2 * P * 4], BF16, name="pair_grouped", align_bytes=256)
             for g in range(PASSES):
                 bank = turn((2 * k, 2 * k + 1), g)
                 empty(bank, pair_grouped[k][:, 1024 * g : 1024 * (g + 1)])
@@ -203,7 +203,7 @@ def tile_transition_density_grid_s2_kernel(tc, phi, p, w, out):
                     phi_codes[2 * k + i, 2] = (codes, scales, i * P, E5M2)
 
         def head_turn(g):
-            grouped = stage.tile([P, HEAD * P * 4], BF16, name="head_grouped", align_bytes=64)
+            grouped = stage.tile([P, HEAD * P * 4], BF16, name="head_grouped", align_bytes=256)
             for h in range(2):
                 bank = turn((2 * h, 2 * h + 1), g)
                 if g == 1:
@@ -280,6 +280,10 @@ def tile_transition_density_grid_s2_kernel(tc, phi, p, w, out):
                 if k is not None and n < 2:
                     pair_quantize(k, n)
 
+        def step(t, b):
+            mult(t, b)
+            dot(t, b)
+
         def by_pass(tiles, b, chores):
             for g in range(PASSES):
                 for t in tiles:
@@ -302,9 +306,17 @@ def tile_transition_density_grid_s2_kernel(tc, phi, p, w, out):
         by_pass(range(0, 4), 2, (p_codes_of(2, 2), [], split_chores(7)))
         rounds(6, grid(range(4, 8), 2), [])
         rounds(7, grid(range(8, 12), 2), [])
-        for t in range(12, TILES):
+        for t in range(12, TILES - 1):
             rounds(None, [(t, b) for b in range(BLOCKS)], [])
 
         rho = keep.tile([P, TILES], F32, name="rho")
-        nc.vector.tensor_reduce(out=rho[:], in_=parts[:], op=ALU.add, axis=mybir.AxisListType.X)
+        last = TILES - 1
+        step(last, 0)
+        step(last, 1)
+        mult(last, 2)
+        sums_of_x = keep.tile([P, last], F32, name="sums_of_x")
+        nc.vector.tensor_reduce(out=sums_of_x[:], in_=parts[:, 0:last, :], op=ALU.add, axis=mybir.AxisListType.X)
+        dot(last, 2)
+        nc.vector.tensor_tensor(out=rho[:, 0:last], in0=sums_of_x[:], in1=w_sb[:, 0:last], op=ALU.mult)
+        nc.vector.tensor_reduce(out=rho[:, last:TILES], in_=parts[:, last, :], op=ALU.add, axis=mybir.AxisListType.X)
         nc.sync.dma_start(out=out.rearrange("(p t) -> p t", t=TILES), in_=rho[:])

from contextlib import ExitStack

import concourse.mybir as mybir
from concourse.masks import make_identity

F32 = mybir.dt.float32
BF16 = mybir.dt.bfloat16
U32 = mybir.dt.uint32
U8 = mybir.dt.uint8
E4M3 = mybir.dt.float8_e4m3fn_x4
E5M2 = mybir.dt.float8_e5m2_x4
ALU = mybir.AluOpType

M, N = 2048, 1536
FLOPS = 2 * M * N * N
P = 128
TILES = M // P
K_PASS = 512
PASSES = N // K_PASS
COLS = 512
BLOCKS = N // COLS
HEAD = 4
V_COLS = (320, 0, 0)


def tile_transition_density_grid_s2_kernel(tc, phi, p, w, out):
    nc = tc.nc
    phi_rows = phi.rearrange("(p t) n -> p t n", t=TILES)
    p_rows = p.rearrange("(g p j) n -> g p j n", p=P, j=4)

    with ExitStack() as ctx:
        keep = ctx.enter_context(tc.tile_pool(name="keep", bufs=1))
        stage = ctx.enter_context(tc.tile_pool(name="stage", bufs=3))
        junk = ctx.enter_context(tc.tile_pool(name="junk", bufs=3))
        turns = ctx.enter_context(tc.psum_pool(name="turns", bufs=3))
        sums = ctx.enter_context(tc.psum_pool(name="sums", bufs=5))
        ctx.enter_context(tc.manual_schedule())

        warm = keep.tile([P, 2], F32, name="warm")
        nc.vector.memset(warm[:], 0.0)
        nc.scalar.copy(out=warm[:, 1:2], in_=warm[:, 0:1])
        ident = keep.tile([P, P], F32, name="ident", align_bytes=256)
        make_identity(nc, ident[:])

        head_phi = [keep.tile([P, HEAD, K_PASS], BF16, name="head_phi%d" % g, align_bytes=256) for g in range(PASSES)]
        p_raw = {}
        for b in range(BLOCKS):
            for g in range(PASSES):
                p_raw[g, b] = keep.tile([P, 4, COLS], BF16, name="p_raw_%d_%d" % (g, b), align_bytes=256)
        pair_phi = {}
        for k in range(2, TILES // 2):
            pair_phi[k] = keep.tile([P, 2, N], BF16, name="pair_phi%d" % k, align_bytes=256)
        def load_head(g):
            cols = slice(g * K_PASS, (g + 1) * K_PASS)
            for t in range(0, HEAD, 2):
                nc.sync.dma_start(out=head_phi[g][:, t : t + 2, :], in_=phi_rows[:, t : t + 2, cols])

        def load_pair(k):
            nc.sync.dma_start(out=pair_phi[k][:], in_=phi_rows[:, 2 * k : 2 * k + 2, :])

        def load_p(g, b):
            nc.sync.dma_start(out=p_raw[g, b][:], in_=p_rows[g, :, :, b * COLS : (b + 1) * COLS])

        w_sb = keep.tile([P, TILES], BF16, name="w_sb")
        for g in range(PASSES):
            load_head(g)
            load_p(g, 0)
        load_pair(2)
        nc.sync.dma_start(out=w_sb[:], in_=w.rearrange("(p t) -> p t", t=TILES))
        load_pair(3)
        load_pair(4)
        load_p(0, 1)
        load_pair(5)
        load_p(1, 1)
        load_p(2, 1)
        for g in range(PASSES):
            load_p(g, 2)
        load_pair(6)
        load_pair(7)

        def phi_part(t, g):
            if t < HEAD:
                return head_phi[g][:, t, :]
            return pair_phi[t // 2][:, t % 2, g * K_PASS : (g + 1) * K_PASS]

        p_codes = {}
        p_scales = {}
        p_grouped = {}

        def p_source(g, b, c0, c1):
            return p_raw[g, b][:, :, c0:c1]

        def p_interleave(engine, g, b, c0, c1):
            if (g, b) not in p_grouped:
                p_grouped[g, b] = stage.tile([P, 4 * COLS], BF16, name="p_grouped", align_bytes=256)
            dst = p_grouped[g, b][:, 4 * c0 : 4 * c1].rearrange("p (c i t) -> p c t i", i=4, t=4)
            src = p_source(g, b, c0, c1).rearrange("p t (c i) -> p c t i", i=4)
            if engine == "v":
                nc.vector.tensor_copy(out=dst, in_=src)
            else:
                nc.scalar.copy(out=dst, in_=src)

        def p_quantize(g, b):
            codes = keep.tile([P, COLS], U32, name="p_codes_%d_%d" % (g, b), align_bytes=256)
            scales = keep.tile([P, COLS], U8, name="p_scales_%d_%d" % (g, b), align_bytes=256)
            nc.vector.quantize_mx(out=codes[:].bitcast(E4M3), scales=scales[:], in_=p_grouped[g, b][:])
            p_codes[g, b] = codes
            p_scales[g, b] = scales

        phi_codes = {}
        phi_scales = {}

        split = {}

        def split_words(k, i):
            if k not in split:
                split[k] = stage.tile([P, 2, PASSES, 2, P], F32, name="split", align_bytes=256)
            nc.scalar.copy(
                out=split[k][:, i, :, :, :],
                in_=pair_phi[k][:, i, :].bitcast(F32).rearrange("p (g m u) -> p g u m", g=PASSES, u=2),
            )

        def turn(tiles, g):
            bank = turns.tile([P, 2, 2, P], F32, name="bank")
            for i in range(2):
                if tiles[i] // 2 in split:
                    halves = [split[tiles[i] // 2][:, i, g, u, :] for u in range(2)]
                else:
                    words = phi_part(tiles[i], g).bitcast(F32)
                    halves = [words[:, u : K_PASS // 2 : 2] for u in range(2)]
                for u in range(2):
                    nc.tensor.transpose(bank[:, i, u, :], halves[u], ident[:])
            return bank

        def empty(bank, dst):
            nc.scalar.copy(
                out=dst.bitcast(F32).rearrange("p (i r u) -> p i r u", i=2, u=2),
                in_=bank[:].rearrange("p i u r -> p i r u"),
            )

        def quantize_phi(src, n_tiles, fmt, label):
            codes = keep.tile([P, n_tiles * P], U32, name="phi_codes_" + label, align_bytes=256)
            scales = keep.tile([P, n_tiles * P], U8, name="phi_scales_" + label, align_bytes=256)
            nc.vector.quantize_mx(out=codes[:].bitcast(fmt), scales=scales[:], in_=src)
            return codes, scales

        accs = {}

        zeros = keep.tile([P, COLS], BF16, name="zeros", align_bytes=256)
        nc.vector.memset(zeros[:], 0.0)

        def keep_clock(n):
            acc = sums.tile([P, COLS], F32, name="acc")
            for i in range(n):
                nc.tensor.matmul(acc[:], lhsT=zeros[:, 0:P], rhs=zeros[:], start=True, stop=True)

        def mult(t, b, passes=(0, 1, 2)):
            if 0 in passes:
                accs[t, b] = sums.tile([P, COLS], F32, name="acc")
            for g in passes:
                codes, scales, col, fmt = phi_codes[t, g]
                nc.tensor.matmul_mx(
                    out=accs[t, b][:],
                    lhsT=codes[:, col : col + P].bitcast(fmt),
                    lhsT_scale=scales[:, col : col + P],
                    rhs=p_codes[g, b][:].bitcast(E4M3),
                    rhs_scale=p_scales[g, b][:],
                    start=(g == 0),
                    stop=(g == PASSES - 1),
                )

        parts = keep.tile([P, TILES, BLOCKS], F32, name="parts")

        def dot(t, b):
            product = junk.tile([P, COLS], F32, name="product")
            nc.vector.scalar_tensor_tensor(
                out=product[:],
                in0=accs[t, b][:],
                scalar=w_sb[:, t : t + 1] if t == TILES - 1 else 1.0,
                in1=phi_part(t, b),
                op0=ALU.mult,
                op1=ALU.mult,
                accum_out=parts[:, t, b : b + 1],
            )

        pair_grouped = {}

        def pair_turn(k):
            pair_grouped[k] = stage.tile([P, 3 * 2 * P * 4], BF16, name="pair_grouped", align_bytes=256)
            for g in range(PASSES):
                bank = turn((2 * k, 2 * k + 1), g)
                empty(bank, pair_grouped[k][:, 1024 * g : 1024 * (g + 1)])

        def pair_quantize(k, which):
            if which == 0:
                codes, scales = quantize_phi(pair_grouped[k][:, 0:2048], 4, E4M3, "a%d" % k)
                for i in range(2):
                    for g in range(2):
                        phi_codes[2 * k + i, g] = (codes, scales, (2 * g + i) * P, E4M3)
            else:
                codes, scales = quantize_phi(pair_grouped[k][:, 2048:3072], 2, E5M2, "b%d" % k)
                for i in range(2):
                    phi_codes[2 * k + i, 2] = (codes, scales, i * P, E5M2)

        def head_turn(g):
            grouped = stage.tile([P, HEAD * P * 4], BF16, name="head_grouped", align_bytes=256)
            for h in range(2):
                bank = turn((2 * h, 2 * h + 1), g)
                if g == 1:
                    keep_clock(1)
                empty(bank, grouped[:, 1024 * h : 1024 * (h + 1)])
            return grouped

        def head_quantize(grouped, g):
            fmt = E4M3 if g < 2 else E5M2
            codes, scales = quantize_phi(grouped[:], HEAD, fmt, "h%d" % g)
            for t in range(HEAD):
                phi_codes[t, g] = (codes, scales, t * P, fmt)

        def p_head(g):
            p_interleave("v", g, 0, 0, V_COLS[0])
            p_interleave("s", g, 0, V_COLS[0], COLS)

        keep_clock(6)
        g0 = head_turn(0)
        keep_clock(3)
        p_head(0)
        head_quantize(g0, 0)
        p_quantize(0, 0)
        g1 = head_turn(1)
        p_head(1)
        head_quantize(g1, 1)
        p_quantize(1, 0)
        for t in range(HEAD):
            mult(t, 0, (0,))
        g2 = head_turn(2)
        p_head(2)
        head_quantize(g2, 2)
        p_quantize(2, 0)
        for t in range(HEAD):
            mult(t, 0, (1,))
        pair_turn(2)
        pair_quantize(2, 0)
        pair_quantize(2, 1)
        for t in range(HEAD):
            mult(t, 0, (2,))
            dot(t, 0)
        pair_turn(3)
        pair_quantize(3, 0)
        pair_quantize(3, 1)

        def p_copies(g, b):
            c0 = V_COLS[b]
            cut = c0 + (COLS - c0) // 2
            calls = [
                lambda: p_interleave("s", g, b, c0, cut),
                lambda: p_interleave("s", g, b, cut, COLS),
            ]
            if c0:
                calls.append(lambda: p_interleave("v", g, b, 0, c0))
            return calls

        def p_codes_of(g, b):
            return [lambda: p_quantize(g, b)]

        def split_chores(k):
            return [lambda: split_words(k, 0), lambda: split_words(k, 1)]

        def rounds(k, groups, chores):
            if k is not None:
                pair_turn(k)
            marks = [(n + 1) * len(chores) // len(groups) for n in range(len(groups))]
            done = 0
            for n in range(len(groups)):
                mult(groups[n][0], groups[n][1])
                for call in chores[done : marks[n]]:
                    call()
                done = marks[n]
                dot(groups[n][0], groups[n][1])
                if k is not None and n < 2:
                    pair_quantize(k, n)

        def step(t, b):
            mult(t, b)
            dot(t, b)

        def by_pass(tiles, b, chores):
            for g in range(PASSES):
                for t in tiles:
                    mult(t, b, (g,))
                    if g == PASSES - 1:
                        dot(t, b)
                for call in chores[g]:
                    call()

        def grid(tiles, b):
            return [(t, b) for t in tiles]

        rounds(4, grid((4, 5), 0), p_copies(0, 1))
        rounds(5, grid((6, 7), 0), p_codes_of(0, 1) + p_copies(1, 1))
        rounds(None, grid((8, 9), 0), p_codes_of(1, 1) + p_copies(2, 1))
        rounds(None, grid((10, 11), 0), [])
        by_pass(range(0, 4), 1, (p_codes_of(2, 1), [], p_copies(0, 2)))
        rounds(None, grid(range(4, 8), 1), p_copies(1, 2) + p_codes_of(0, 2))
        rounds(None, grid(range(8, 12), 1), p_codes_of(1, 2) + p_copies(2, 2) + split_chores(6))
        by_pass(range(0, 4), 2, (p_codes_of(2, 2), [], split_chores(7)))
        rounds(6, grid(range(4, 8), 2), [])
        rounds(7, grid(range(8, 12), 2), [])
        for t in range(12, TILES - 1):
            rounds(None, [(t, b) for b in range(BLOCKS)], [])

        rho = keep.tile([P, TILES], F32, name="rho")
        last = TILES - 1
        step(last, 0)
        step(last, 1)
        mult(last, 2)
        sums_of_x = keep.tile([P, last], F32, name="sums_of_x")
        nc.vector.tensor_reduce(out=sums_of_x[:], in_=parts[:, 0:last, :], op=ALU.add, axis=mybir.AxisListType.X)
        dot(last, 2)
        nc.vector.tensor_tensor(out=rho[:, 0:last], in0=sums_of_x[:], in1=w_sb[:, 0:last], op=ALU.mult)
        nc.vector.tensor_reduce(out=rho[:, last:TILES], in_=parts[:, last, :], op=ALU.add, axis=mybir.AxisListType.X)
        nc.sync.dma_start(out=out.rearrange("(p t) -> p t", t=TILES), in_=rho[:])
